import numpy as np
import ml_dtypes


def mxq(x, axis, fmt="e4m3"):
    dtype, down = {"e4m3": (ml_dtypes.float8_e4m3fn, 7), "e5m2": (ml_dtypes.float8_e5m2, 14)}[fmt]
    v = np.moveaxis(np.asarray(x, np.float32).astype(ml_dtypes.bfloat16).astype(np.float64), axis, -1)
    blocks = v.reshape(v.shape[:-1] + (-1, 32))
    amax = np.abs(blocks).max(-1, keepdims=True)
    byte = np.maximum(np.where(amax > 0, np.frexp(amax)[1] - 1 + 127, 0) - down, 1)
    scale = np.exp2(byte - 127.0)
    codes = (blocks / scale).astype(np.float32).astype(dtype).astype(np.float64)
    return np.moveaxis((codes * scale).reshape(v.shape), -1, axis)


WIDE = False


def mx_kscale(k):
    if not WIDE:
        return np.ones(k)
    levels = np.array([10, -10, 5, -5, 0])
    if k % 512:
        return np.exp2(np.random.permutation(np.resize(levels, k // 32))).repeat(32)
    a = np.empty((k // 512, 16))
    for p in range(k // 512):
        a[p, :8] = np.random.permutation(np.resize(levels, 8))
        for g in range(8):
            far = levels[np.abs(levels - a[p, g]) >= 10]
            a[p, g + 8] = far[np.random.randint(len(far))]
    return np.exp2(a.ravel()).repeat(32)


def f64(x):
    return np.asarray(x).astype(np.float64)


def striped(idx):
    return np.tile(idx.reshape(-1, 16).T, (8, 1)).astype(np.uint16)


def unstriped(offs):
    return offs[:16].T.reshape(-1).astype(np.int64)


E2M1 = np.array([0.0, 0.5, 1.0, 1.5, 2.0, 3.0, 4.0, 6.0, -0.0, -0.5, -1.0, -1.5, -2.0, -3.0, -4.0, -6.0])


def pack_weight(w, fmt):
    k, n = w.shape
    w = f64(np.asarray(w, np.float32).astype(ml_dtypes.bfloat16)).reshape(k // 32, 32, n)
    amax = np.abs(w).max(1)
    if fmt == "e4m3":
        byte = np.frexp(amax)[1] - 1 + 127 - 7
    else:
        mant, ex = np.frexp(amax / 6.0)
        byte = np.where(mant > 0.5, ex, ex - 1) + 127
    byte = np.clip(np.where(amax > 0, byte, 1), 1, 254)
    scaled = (w * np.exp2(127.0 - byte)[:, None, :]).reshape(k, n).astype(np.float32)
    by_word = np.ascontiguousarray(scaled.reshape(k // 512, 128, 4, n).transpose(0, 1, 3, 2))
    if fmt == "e4m3":
        words = by_word.astype(ml_dtypes.float8_e4m3fn).view(np.uint8)
    else:
        c = by_word.astype(ml_dtypes.float4_e2m1fn).view(np.uint8) & 0xF
        words = (c[..., 0::2] | (c[..., 1::2] << 4)).reshape(k // 512, 128, 2 * n)
    return np.ascontiguousarray(words), np.ascontiguousarray(byte.astype(np.uint8).reshape(k // 512, 16, n))


def unpack_weight(words, scales, fmt):
    g, _, n = scales.shape
    words = np.ascontiguousarray(words).reshape(g, 128, n, -1)
    if fmt == "e4m3":
        vals = words.view(ml_dtypes.float8_e4m3fn).astype(np.float64)
    else:
        nib = np.empty((g, 128, n, 4), np.uint8)
        nib[..., 0::2] = words & 0xF
        nib[..., 1::2] = words >> 4
        vals = E2M1[nib]
    vals = vals * np.repeat(np.exp2(scales.astype(np.float64) - 127.0), 8, axis=1)[..., None]
    return vals.transpose(0, 1, 3, 2).reshape(g * 512, n)


def gelu(v):
    return 0.5 * v * (1.0 + np.tanh(np.sqrt(2.0 / np.pi) * (v + 0.044715 * v**3)))


K, K2, H, N, T, S = 512, 1024, 1024, 384, 2048, 1024


def setup_inputs():
    n = np.random.standard_normal
    s = mx_kscale(K)[:, None]
    s2 = mx_kscale(K2)[:, None]
    u = mx_kscale(H)[:, None]
    d = {}
    d["tab_words"], d["tab_scales"] = pack_weight(n((K, T)) * s, "e4m3")
    d["offs"] = striped(np.random.permutation(T)[:S])
    d["xs_words"], d["xs_scales"] = pack_weight(n((K2, S)) * s2, "e4m3")
    d["w1"] = (n((K, H)) / s * u.T / K ** 0.5).astype(np.float32)
    d["w2_words"], d["w2_scales"] = pack_weight(n((K, H)) / s * u.T / K ** 0.5, "e2m1")
    d["wx"] = (n((K2, H)) / s2 * u.T / K2 ** 0.5).astype(np.float32)
    d["bx"] = (0.6 * n(H) * u[:, 0]).astype(np.float32)
    d["wo"] = (1.4 * n((H, N)) / u / H ** 0.5).astype(np.float32)
    d["bo"] = (0.5 * n(N)).astype(np.float32)
    return d


def reference(tab_words, tab_scales, offs, xs_words, xs_scales, w1, w2_words, w2_scales, wx, bx, wo, bo):
    v = unpack_weight(tab_words, tab_scales, "e4m3")[:, unstriped(offs)]
    xs = unpack_weight(xs_words, xs_scales, "e4m3")
    w2 = unpack_weight(w2_words, w2_scales, "e2m1")
    l1 = mxq(f64(w1), 0, "e4m3").T @ v
    l2 = w2.T @ v
    l3 = (mxq(f64(wx), 0, "e4m3").T @ xs) + f64(bx)[:, None]
    low = np.minimum(l1, l2)
    high = np.maximum(l1, l2)
    h = np.maximum(low, np.minimum(l3, high))
    y = mxq(f64(wo), 0, "e4m3").T @ mxq(h, 0, "e4m3")
    return y + f64(bo)[:, None]

@@ -1,0 +1,306 @@
+from contextlib import ExitStack
+
+import concourse.mybir as mybir
+from concourse.masks import make_identity
+
+K, K2, H, N, T, S = 512, 1024, 1024, 384, 2048, 1024
+FLOPS = 2 * S * H * (K + K + K2 + N)
+
+F32 = mybir.dt.float32
+BF16 = mybir.dt.bfloat16
+I32 = mybir.dt.int32
+U32 = mybir.dt.uint32
+U16 = mybir.dt.uint16
+U8 = mybir.dt.uint8
+FP8X4 = mybir.dt.float8_e4m3fn_x4
+FP4X4 = mybir.dt.float4_e2m1fn_x4
+ALU = mybir.AluOpType
+IDENTITY = mybir.ActivationFunctionType.Identity
+
+P = 128
+PACK = 4
+PASS = 512
+BANK = 512
+GROUPS = H // PASS
+HALVES = S // BANK
+N_TILES = N // P
+BO = GROUPS * PACK
+
+
+def tile_list_drum_level_median_kernel(
+    tc, tab_words, tab_scales, offs, xs_words, xs_scales, w1, w2_words, w2_scales, wx, bx, wo, bo, out
+):
+    nc = tc.nc
+    with ExitStack() as ctx:
+        keep = ctx.enter_context(tc.tile_pool(name="keep", bufs=1))
+        ring = ctx.enter_context(tc.tile_pool(name="ring", bufs=2))
+        psum = ctx.enter_context(tc.psum_pool(name="psum", bufs=2))
+
+        def held(name, shape, dtype):
+            return keep.tile(shape, dtype, name=name, align_bytes=64)
+
+        offsets = keep.tile([P, S // 16], U16, name="offsets")
+        tab_w = held("tab_w", [P, T], U32)
+        tab_s = held("tab_s", [P, T], U8)
+        w2_raw_w = held("w2_raw_w", [P, H // 2], I32)
+        w2_raw_s = held("w2_raw_s", [P, H // 4], I32)
+        w2_w = held("w2_w", [P, 2 * H], U8)
+        w2_s = held("w2_s", [P, H], U8)
+        xs_w = [held("xs_w%d" % a, [P, S], U32) for a in range(2)]
+        xs_s = held("xs_s", [P, S], U8)
+        bias_rows = held("bias_rows", [P, P], F32)
+        identity = held("identity", [P, P], F32)
+        bias = held("bias", [P, 16], F32)
+        nc.gpsimd.memset(bias_rows[:], 0.0)
+        make_identity(nc, identity[:])
+
+        nc.vector.memset(tab_s[:].bitcast(I32), 0)
+        nc.vector.memset(w2_raw_s[:], 0)
+        nc.vector.memset(xs_s[:].bitcast(I32), 0)
+
+        def load_weight(src, a, g):
+            raw = ring.tile([P, PACK, PASS], F32, name="w_raw", tag="w_raw", bufs=5, align_bytes=64)
+            rows = src[a * PASS : (a + 1) * PASS, g * PASS : (g + 1) * PASS]
+            nc.sync.dma_start(out=raw[:], in_=rows.rearrange("(p j) c -> p j c", j=PACK))
+            return raw
+
+        nc.sync.dma_start(offsets[:], offs)
+        nc.sync.dma_start(out=tab_w[:].bitcast(I32), in_=tab_words[0].rearrange("p t i -> p (t i)").bitcast(I32))
+        for q in range(4):
+            nc.sync.dma_start(
+                out=tab_s[32 * q : 32 * q + 4, :].bitcast(I32), in_=tab_scales[0, 4 * q : 4 * q + 4, :].bitcast(I32)
+            )
+        nc.sync.dma_start(out=w2_raw_w[:], in_=w2_words[0].bitcast(I32))
+        for q in range(4):
+            nc.sync.dma_start(out=w2_raw_s[32 * q : 32 * q + 4, :], in_=w2_scales[0, 4 * q : 4 * q + 4, :].bitcast(I32))
+        w1_raw = {0: load_weight(w1, 0, 0)}
+        wx_raw = {(a, 0): load_weight(wx, a, 0) for a in range(2)}
+        for a in range(2):
+            nc.sync.dma_start(out=xs_w[a][:].bitcast(I32), in_=xs_words[a].rearrange("p c i -> p (c i)").bitcast(I32))
+        for q in range(4):
+            nc.sync.dma_start(
+                out=xs_s[32 * q : 32 * q + 8, :].bitcast(I32), in_=xs_scales[:, 4 * q : 4 * q + 4, :].bitcast(I32)
+            )
+        bx_by_slot = bx.rearrange("(g u t i) -> g t u i", g=GROUPS, t=PACK, i=4)
+        for g in range(GROUPS):
+            nc.sync.dma_start(
+                out=bias_rows[g * PACK : (g + 1) * PACK, :].rearrange("t (u i) -> t u i", i=4), in_=bx_by_slot[g]
+            )
+        nc.sync.dma_start(out=bias_rows[BO : BO + N_TILES, :], in_=bo.rearrange("(a p) -> a p", p=P))
+        w1_raw[1] = load_weight(w1, 0, 1)
+        for a in range(2):
+            wx_raw[(a, 1)] = load_weight(wx, a, 1)
+        wo_raw = [held("wo_raw%d" % g, [P, PACK, N], F32) for g in range(GROUPS)]
+        wo_by_slot = wo.rearrange("(g u t i) n -> g t u i n", g=GROUPS, t=PACK, i=4)
+        for g in range(GROUPS):
+            for t in range(PACK):
+                nc.sync.dma_start(out=wo_raw[g][:, t, :], in_=wo_by_slot[g, t])
+
+        v_w = [held("v_w%d" % h, [P, BANK], U32) for h in range(HALVES)]
+        v_s = [held("v_s%d" % h, [P, BANK], U8) for h in range(HALVES)]
+
+        def gather(h):
+            picks = offsets[:, h * (BANK // 16) : (h + 1) * (BANK // 16)]
+            nc.vector.tensor_copy(v_w[h][:], tab_w[:].indirect(picks))
+            nc.vector.tensor_copy(v_s[h][:], tab_s[:].indirect(picks))
+
+        def deal_w2():
+            nc.vector.tensor_copy(
+                out=w2_w[:].bitcast(I32).rearrange("p (g t u e) -> p g t u e", g=GROUPS, t=PACK, e=2),
+                in_=w2_raw_w[:].rearrange("p (g u t e) -> p g t u e", g=GROUPS, t=PACK, e=2),
+            )
+            nc.vector.tensor_copy(
+                out=w2_s[:].bitcast(I32).rearrange("p (g t u) -> p g t u", g=GROUPS, t=PACK),
+                in_=w2_raw_s[:].rearrange("p (g u t) -> p g t u", g=GROUPS, t=PACK),
+            )
+
+        def weave_weight(raw):
+            woven = ring.tile([P, PACK * PASS], BF16, name="woven", tag="woven", bufs=3, align_bytes=64)
+            dst = woven[:].rearrange("p (t u i j) -> p t u i j", t=PACK, i=4, j=PACK)
+            src = raw[:].rearrange("p j (u t i) -> p t u i j", t=PACK, i=4)
+            for t in range(PACK):
+                nc.scalar.copy(out=dst[:, t], in_=src[:, t])
+            return woven
+
+        def quantise(name, woven, pieces):
+            cols = sum(pieces) // PACK
+            codes = held(name + "_w", [P, cols], U32)
+            scales = held(name + "_s", [P, cols], U8)
+            at = 0
+            steps = []
+            for width in pieces:
+                c = slice(at // PACK, (at + width) // PACK)
+                steps.append(
+                    lambda c=c, at=at, width=width: nc.vector.quantize_mx(
+                        out=codes[:, c].bitcast(FP8X4), scales=scales[:, c], in_=woven[:, at : at + width]
+                    )
+                )
+                at = at + width
+            return (codes, scales), steps
+
+        w1_q, wx_q = {}, {}
+        low, high, mid, voted, h_q = {}, {}, {}, {}, {}
+
+        def low_high(g, h, t):
+            cols = slice(t * P, (t + 1) * P)
+            c0 = g * PASS + t * P
+            l2_ps = psum.tile([P, BANK], F32, name="l2_ps", tag="scalar_side", bufs=3)
+            nc.tensor.matmul_mx(
+                out=l2_ps[:],
+                lhsT=w2_w[:, 2 * c0 : 2 * (c0 + P)].bitcast(FP4X4),
+                lhsT_scale=w2_s[:, c0 : c0 + P],
+                rhs=v_w[h][:].bitcast(FP8X4),
+                rhs_scale=v_s[h][:],
+                start=True,
+                stop=True,
+            )
+            l2 = ring.tile([P, BANK], F32, name="l2", tag="l2", bufs=4)
+            nc.scalar.copy(out=l2[:], in_=l2_ps[:])
+            l1_ps = psum.tile([P, BANK], F32, name="l1_ps", tag="l1", bufs=2)
+            codes, scales = w1_q[g]
+            nc.tensor.matmul_mx(
+                out=l1_ps[:],
+                lhsT=codes[:, cols].bitcast(FP8X4),
+                lhsT_scale=scales[:, cols],
+                rhs=v_w[h][:].bitcast(FP8X4),
+                rhs_scale=v_s[h][:],
+                start=True,
+                stop=True,
+            )
+            if t == 0:
+                low[(g, h)] = ring.tile([P, PACK, BANK], F32, name="low", tag="low", bufs=3)
+            high[(g, h, t)] = ring.tile([P, BANK], F32, name="high", tag="high", bufs=8)
+            nc.vector.tensor_tensor(out=low[(g, h)][:, t, :], in0=l1_ps[:], in1=l2[:], op=ALU.min)
+            nc.vector.tensor_tensor(out=high[(g, h, t)][:], in0=l1_ps[:], in1=l2[:], op=ALU.max)
+
+        def cap(g, h, t):
+            cols = slice(t * P, (t + 1) * P)
+            toks = slice(h * BANK, (h + 1) * BANK)
+            l3_ps = psum.tile([P, BANK], F32, name="l3_ps", tag="l3", bufs=3)
+            for a in range(2):
+                codes, scales = wx_q[(a, g)]
+                nc.tensor.matmul_mx(
+                    out=l3_ps[:],
+                    lhsT=codes[:, cols].bitcast(FP8X4),
+                    lhsT_scale=scales[:, cols],
+                    rhs=xs_w[a][:, toks].bitcast(FP8X4),
+                    rhs_scale=xs_s[4 * a : P, toks],
+                    start=(a == 0),
+                    stop=(a == 1),
+                )
+            if t == 0:
+                mid[(g, h)] = ring.tile([P, PACK, BANK], F32, name="mid", tag="mid", bufs=2)
+            nc.vector.scalar_tensor_tensor(
+                out=mid[(g, h)][:, t, :],
+                in0=l3_ps[:],
+                scalar=bias[:, g * PACK + t : g * PACK + t + 1],
+                in1=high[(g, h, t)][:],
+                op0=ALU.add,
+                op1=ALU.min,
+            )
+
+        def vote(g, h, c0, width):
+            if c0 == 0:
+                voted[(g, h)] = ring.tile([P, PACK * BANK], BF16, name="voted", tag="voted", bufs=2, align_bytes=64)
+            walk = "p t (c i) -> p c t i"
+            nc.vector.tensor_tensor(
+                out=voted[(g, h)][:, PACK * c0 : PACK * (c0 + width)].rearrange("p (c i t) -> p c t i", i=4, t=PACK),
+                in0=low[(g, h)][:, :, c0 : c0 + width].rearrange(walk, i=4),
+                in1=mid[(g, h)][:, :, c0 : c0 + width].rearrange(walk, i=4),
+                op=ALU.max,
+            )
+
+        def quantise_h(g, h, c0, width):
+            if (g, h) not in h_q:
+                h_q[(g, h)] = (held("h_w%d%d" % (g, h), [P, BANK], U32), held("h_s%d%d" % (g, h), [P, BANK], U8))
+            codes, scales = h_q[(g, h)]
+            nc.vector.quantize_mx(
+                out=codes[:, c0 : c0 + width].bitcast(FP8X4), scales=scales[:, c0 : c0 + width], in_=voted[(g, h)][:, PACK * c0 : PACK * (c0 + width)]
+            )
+
+        def scores(h, c0, width, banks):
+            staged = held("staged%d_%d" % (h, c0), [P, N_TILES, width], F32)
+            codes, scales = wo_q
+            for n in range(N_TILES):
+                y_ps = psum.tile([P, width], F32, name="y_ps", tag=banks, bufs=3)
+                for g in range(GROUPS):
+                    cols = slice(g * N + n * P, g * N + (n + 1) * P)
+                    nc.tensor.matmul_mx(
+                        out=y_ps[:],
+                        lhsT=codes[:, cols].bitcast(FP8X4),
+                        lhsT_scale=scales[:, cols],
+                        rhs=h_q[(g, h)][0][:, c0 : c0 + width].bitcast(FP8X4),
+                        rhs_scale=h_q[(g, h)][1][:, c0 : c0 + width],
+                        start=(g == 0),
+                        stop=(g == GROUPS - 1),
+                    )
+                nc.scalar.activation(out=staged[:, n, :], in_=y_ps[:], func=IDENTITY, bias=bias[:, BO + n : BO + n + 1])
+            j0 = h * BANK + c0
+            nc.sync.dma_start(out=out[:, j0 : j0 + width].rearrange("(a p) j -> p a j", p=P), in_=staged[:])
+
+        HB = BANK // 2
+
+        gather(0)
+        deal_w2()
+        gather(1)
+        w1_q[0], steps = quantise("w1q0", weave_weight(w1_raw[0]), [512] * 4)
+        for t in range(PACK):
+            steps[t]()
+            if t > 0:
+                low_high(0, 0, t - 1)
+        low_high(0, 0, 3)
+        wx_q[(0, 0)], steps0 = quantise("wxq00", weave_weight(wx_raw[(0, 0)]), [2048])
+        low_high(0, 1, 0)
+        steps0[0]()
+        low_high(0, 1, 1)
+        wx_q[(1, 0)], steps1 = quantise("wxq10", weave_weight(wx_raw[(1, 0)]), [2048])
+        low_high(0, 1, 2)
+        steps1[0]()
+        bias_ps = psum.tile([P, P], F32, name="bias_ps", tag="scalar_side", bufs=3)
+        nc.tensor.transpose(bias_ps[:], bias_rows[:], identity[:])
+        nc.scalar.copy(out=bias[:], in_=bias_ps[:, 0:16])
+        low_high(0, 1, 3)
+
+        w1_q[1], steps = quantise("w1q1", weave_weight(w1_raw[1]), [2048])
+        for t in range(PACK):
+            cap(0, 0, t)
+        steps[0]()
+        wx_q[(0, 1)], steps0 = quantise("wxq01", weave_weight(wx_raw[(0, 1)]), [2048])
+        wx_q[(1, 1)], steps1 = quantise("wxq11", weave_weight(wx_raw[(1, 1)]), [2048])
+
+        def finish(g, h, between):
+            between[0]()
+            vote(g, h, 0, HB)
+            between[1]()
+            vote(g, h, HB, HB)
+            between[2]()
+            quantise_h(g, h, 0, BANK)
+            between[3]()
+
+        finish(0, 0, [lambda t=t: cap(0, 1, t) for t in range(PACK)])
+        finish(0, 1, [lambda t=t: low_high(1, 0, t) for t in range(PACK)])
+        steps0[0]()
+        low_high(1, 1, 0)
+        steps1[0]()
+        wo_woven = held("wo_woven", [P, GROUPS * N * PACK], BF16)
+        for g in range(GROUPS):
+            dst = wo_woven[:, g * N * PACK : (g + 1) * N * PACK].rearrange("p (n t) -> p n t", t=PACK)
+            src = wo_raw[g][:].rearrange("p t n -> p n t")
+            for n in range(N_TILES):
+                nc.scalar.copy(out=dst[:, n * P : (n + 1) * P], in_=src[:, n * P : (n + 1) * P])
+        wo_q, steps = quantise("woq", wo_woven, [2048, 1024])
+        for t in range(PACK):
+            cap(1, 0, t)
+            if t < PACK - 1:
+                low_high(1, 1, t + 1)
+        steps[0]()
+        steps[1]()
+        finish(1, 0, [lambda t=t: cap(1, 1, t) for t in range(PACK)])
+        scores(0, 0, BANK, "scalar_side")
+        tail = [(0, 256), (256, 128), (384, 128)]
+        vote(1, 1, *tail[0])
+        for k in range(len(tail)):
+            if k + 1 < len(tail):
+                vote(1, 1, *tail[k + 1])
+            quantise_h(1, 1, tail[k][0], tail[k][1])
+            scores(1, tail[k][0], tail[k][1], ["l3", "scalar_side"][k % 2])

@@ -43,7 +43,7 @@ def tile_list_drum_level_median_kernel(
         tab_w = held("tab_w", [P, T], U32)
         tab_s = held("tab_s", [P, T], U8)
         w2_raw_w = held("w2_raw_w", [P, H // 2], I32)
-        w2_raw_s = held("w2_raw_s", [P, H // 4], I32)
+        w2_raw_s = keep.tile([P, H // 4], I32, name="w2_raw_s", tag="scales_twice", align_bytes=64)
         w2_w = held("w2_w", [P, 2 * H], U8)
         w2_s = held("w2_s", [P, H], U8)
         xs_w = [held("xs_w%d" % a, [P, S], U32) for a in range(2)]
@@ -51,43 +51,46 @@ def tile_list_drum_level_median_kernel(
         bias_rows = held("bias_rows", [P, P], F32)
         identity = held("identity", [P, P], F32)
         bias = held("bias", [P, 16], F32)
-        nc.gpsimd.memset(bias_rows[:], 0.0)
-        make_identity(nc, identity[:])
 
         nc.vector.memset(tab_s[:].bitcast(I32), 0)
         nc.vector.memset(w2_raw_s[:], 0)
         nc.vector.memset(xs_s[:].bitcast(I32), 0)
+        nc.vector.memset(bias_rows[:], 0.0)
+        nc.vector.memset(identity[:], 0.0)
 
         def load_weight(src, a, g):
-            raw = ring.tile([P, PACK, PASS], F32, name="w_raw", tag="w_raw", bufs=5, align_bytes=64)
+            raw = ring.tile([P, PACK, PASS], F32, name="w_raw", tag="w_raw", bufs=4, align_bytes=64)
             rows = src[a * PASS : (a + 1) * PASS, g * PASS : (g + 1) * PASS]
             nc.sync.dma_start(out=raw[:], in_=rows.rearrange("(p j) c -> p j c", j=PACK))
             return raw
 
-        nc.sync.dma_start(offsets[:], offs)
         nc.sync.dma_start(out=tab_w[:].bitcast(I32), in_=tab_words[0].rearrange("p t i -> p (t i)").bitcast(I32))
+        nc.sync.dma_start(offsets[:], offs)
         for q in range(4):
             nc.sync.dma_start(
                 out=tab_s[32 * q : 32 * q + 4, :].bitcast(I32), in_=tab_scales[0, 4 * q : 4 * q + 4, :].bitcast(I32)
             )
+        w1_raw = {0: load_weight(w1, 0, 0)}
         nc.sync.dma_start(out=w2_raw_w[:], in_=w2_words[0].bitcast(I32))
         for q in range(4):
-            nc.sync.dma_start(out=w2_raw_s[32 * q : 32 * q + 4, :], in_=w2_scales[0, 4 * q : 4 * q + 4, :].bitcast(I32))
-        w1_raw = {0: load_weight(w1, 0, 0)}
+            nc.sync.dma_start(
+                out=w2_raw_s[32 * q : 32 * q + 4, :], in_=w2_scales[0, 4 * q : 4 * q + 4, :].bitcast(I32)
+            )
+        make_identity(nc, identity[:], nomemset=True)
         wx_raw = {(a, 0): load_weight(wx, a, 0) for a in range(2)}
         for a in range(2):
             nc.sync.dma_start(out=xs_w[a][:].bitcast(I32), in_=xs_words[a].rearrange("p c i -> p (c i)").bitcast(I32))
-        for q in range(4):
-            nc.sync.dma_start(
-                out=xs_s[32 * q : 32 * q + 8, :].bitcast(I32), in_=xs_scales[:, 4 * q : 4 * q + 4, :].bitcast(I32)
-            )
+            for q in range(2 * a, 2 * a + 2):
+                nc.sync.dma_start(
+                    out=xs_s[32 * q : 32 * q + 8, :].bitcast(I32), in_=xs_scales[:, 4 * q : 4 * q + 4, :].bitcast(I32)
+                )
+        w1_raw[1] = load_weight(w1, 0, 1)
         bx_by_slot = bx.rearrange("(g u t i) -> g t u i", g=GROUPS, t=PACK, i=4)
         for g in range(GROUPS):
             nc.sync.dma_start(
                 out=bias_rows[g * PACK : (g + 1) * PACK, :].rearrange("t (u i) -> t u i", i=4), in_=bx_by_slot[g]
             )
         nc.sync.dma_start(out=bias_rows[BO : BO + N_TILES, :], in_=bo.rearrange("(a p) -> a p", p=P))
-        w1_raw[1] = load_weight(w1, 0, 1)
         for a in range(2):
             wx_raw[(a, 1)] = load_weight(wx, a, 1)
         wo_raw = [held("wo_raw%d" % g, [P, PACK, N], F32) for g in range(GROUPS)]
@@ -96,13 +99,18 @@ def tile_list_drum_level_median_kernel(
             for t in range(PACK):
                 nc.sync.dma_start(out=wo_raw[g][:, t, :], in_=wo_by_slot[g, t])
 
-        v_w = [held("v_w%d" % h, [P, BANK], U32) for h in range(HALVES)]
-        v_s = [held("v_s%d" % h, [P, BANK], U8) for h in range(HALVES)]
+        v_w, v_s = {}, {}
 
-        def gather(h):
-            picks = offsets[:, h * (BANK // 16) : (h + 1) * (BANK // 16)]
-            nc.vector.tensor_copy(v_w[h][:], tab_w[:].indirect(picks))
-            nc.vector.tensor_copy(v_s[h][:], tab_s[:].indirect(picks))
+        def picks(h):
+            return offsets[:, h * (BANK // 16) : (h + 1) * (BANK // 16)]
+
+        def gather_words(h):
+            v_w[h] = held("v_w%d" % h, [P, BANK], U32)
+            nc.vector.tensor_copy(v_w[h][:], tab_w[:].indirect(picks(h)))
+
+        def gather_scales(h, tag):
+            v_s[h] = keep.tile([P, BANK], U8, name="v_s", tag=tag, align_bytes=64)
+            nc.vector.tensor_copy(v_s[h][:], tab_s[:].indirect(picks(h)))
 
         def deal_w2():
             nc.vector.tensor_copy(
@@ -139,7 +147,7 @@ def tile_list_drum_level_median_kernel(
             return (codes, scales), steps
 
         w1_q, wx_q = {}, {}
-        low, high, mid, voted, h_q = {}, {}, {}, {}, {}
+        low, high, mid, voted, h_woven, h_q = {}, {}, {}, {}, {}, {}
 
         def low_high(g, h, t):
             cols = slice(t * P, (t + 1) * P)
@@ -173,10 +181,10 @@ def tile_list_drum_level_median_kernel(
             nc.vector.tensor_tensor(out=low[(g, h)][:, t, :], in0=l1_ps[:], in1=l2[:], op=ALU.min)
             nc.vector.tensor_tensor(out=high[(g, h, t)][:], in0=l1_ps[:], in1=l2[:], op=ALU.max)
 
-        def cap(g, h, t):
+        def cap(g, h, t, c0=0, width=BANK):
             cols = slice(t * P, (t + 1) * P)
-            toks = slice(h * BANK, (h + 1) * BANK)
-            l3_ps = psum.tile([P, BANK], F32, name="l3_ps", tag="l3", bufs=3)
+            toks = slice(h * BANK + c0, h * BANK + c0 + width)
+            l3_ps = psum.tile([P, width], F32, name="l3_ps", tag="l3", bufs=3)
             for a in range(2):
                 codes, scales = wx_q[(a, g)]
                 nc.tensor.matmul_mx(
@@ -188,26 +196,30 @@ def tile_list_drum_level_median_kernel(
                     start=(a == 0),
                     stop=(a == 1),
                 )
-            if t == 0:
+            if t == 0 and c0 == 0:
                 mid[(g, h)] = ring.tile([P, PACK, BANK], F32, name="mid", tag="mid", bufs=2)
             nc.vector.scalar_tensor_tensor(
-                out=mid[(g, h)][:, t, :],
+                out=mid[(g, h)][:, t, c0 : c0 + width],
                 in0=l3_ps[:],
                 scalar=bias[:, g * PACK + t : g * PACK + t + 1],
-                in1=high[(g, h, t)][:],
+                in1=high[(g, h, t)][:, c0 : c0 + width],
                 op0=ALU.add,
                 op1=ALU.min,
             )
 
         def vote(g, h, c0, width):
             if c0 == 0:
-                voted[(g, h)] = ring.tile([P, PACK * BANK], BF16, name="voted", tag="voted", bufs=2, align_bytes=64)
-            walk = "p t (c i) -> p c t i"
+                voted[(g, h)] = ring.tile([P, PACK, BANK], BF16, name="voted", tag="voted", bufs=2)
+                h_woven[(g, h)] = ring.tile([P, PACK * BANK], BF16, name="h_woven", tag="h_woven", bufs=2, align_bytes=64)
+            toks = slice(c0, c0 + width)
             nc.vector.tensor_tensor(
-                out=voted[(g, h)][:, PACK * c0 : PACK * (c0 + width)].rearrange("p (c i t) -> p c t i", i=4, t=PACK),
-                in0=low[(g, h)][:, :, c0 : c0 + width].rearrange(walk, i=4),
-                in1=mid[(g, h)][:, :, c0 : c0 + width].rearrange(walk, i=4),
-                op=ALU.max,
+                out=voted[(g, h)][:, :, toks], in0=low[(g, h)][:, :, toks], in1=mid[(g, h)][:, :, toks], op=ALU.max
+            )
+
+        def weave_h(g, h, c0, width, copy):
+            copy(
+                out=h_woven[(g, h)][:, PACK * c0 : PACK * (c0 + width)].rearrange("p (j t) -> p j t", t=PACK),
+                in_=voted[(g, h)][:, :, c0 : c0 + width].rearrange("p t j -> p j t"),
             )
 
         def quantise_h(g, h, c0, width):
@@ -215,34 +227,45 @@ def tile_list_drum_level_median_kernel(
                 h_q[(g, h)] = (held("h_w%d%d" % (g, h), [P, BANK], U32), held("h_s%d%d" % (g, h), [P, BANK], U8))
             codes, scales = h_q[(g, h)]
             nc.vector.quantize_mx(
-                out=codes[:, c0 : c0 + width].bitcast(FP8X4), scales=scales[:, c0 : c0 + width], in_=voted[(g, h)][:, PACK * c0 : PACK * (c0 + width)]
+                out=codes[:, c0 : c0 + width].bitcast(FP8X4), scales=scales[:, c0 : c0 + width], in_=h_woven[(g, h)][:, PACK * c0 : PACK * (c0 + width)]
             )
 
-        def scores(h, c0, width, banks):
-            staged = held("staged%d_%d" % (h, c0), [P, N_TILES, width], F32)
+        def score_pass(y_ps, n, g, h, c0, width):
             codes, scales = wo_q
+            cols = slice(g * N + n * P, g * N + (n + 1) * P)
+            nc.tensor.matmul_mx(
+                out=y_ps[:],
+                lhsT=codes[:, cols].bitcast(FP8X4),
+                lhsT_scale=scales[:, cols],
+                rhs=h_q[(g, h)][0][:, c0 : c0 + width].bitcast(FP8X4),
+                rhs_scale=h_q[(g, h)][1][:, c0 : c0 + width],
+                start=(g == 0),
+                stop=(g == GROUPS - 1),
+            )
+
+        def open_scores(h, c0, width, tag, bufs):
+            banks = []
             for n in range(N_TILES):
-                y_ps = psum.tile([P, width], F32, name="y_ps", tag=banks, bufs=3)
-                for g in range(GROUPS):
-                    cols = slice(g * N + n * P, g * N + (n + 1) * P)
-                    nc.tensor.matmul_mx(
-                        out=y_ps[:],
-                        lhsT=codes[:, cols].bitcast(FP8X4),
-                        lhsT_scale=scales[:, cols],
-                        rhs=h_q[(g, h)][0][:, c0 : c0 + width].bitcast(FP8X4),
-                        rhs_scale=h_q[(g, h)][1][:, c0 : c0 + width],
-                        start=(g == 0),
-                        stop=(g == GROUPS - 1),
-                    )
-                nc.scalar.activation(out=staged[:, n, :], in_=y_ps[:], func=IDENTITY, bias=bias[:, BO + n : BO + n + 1])
+                y_ps = psum.tile([P, width], F32, name="y_ps", tag=tag, bufs=bufs)
+                score_pass(y_ps, n, 0, h, c0, width)
+                banks.append(y_ps)
+            return banks
+
+        def close_scores(h, c0, width, banks):
+            staged = held("staged%d_%d" % (h, c0), [P, N_TILES, width], F32)
+            for n in range(N_TILES):
+                score_pass(banks[n], n, 1, h, c0, width)
+                nc.scalar.activation(out=staged[:, n, :], in_=banks[n][:], func=IDENTITY, bias=bias[:, BO + n : BO + n + 1])
             j0 = h * BANK + c0
             nc.sync.dma_start(out=out[:, j0 : j0 + width].rearrange("(a p) j -> p a j", p=P), in_=staged[:])
 
         HB = BANK // 2
 
-        gather(0)
+        gather_words(0)
+        gather_scales(0, "v_s0")
+        gather_words(1)
         deal_w2()
-        gather(1)
+        gather_scales(1, "scales_twice")
         w1_q[0], steps = quantise("w1q0", weave_weight(w1_raw[0]), [512] * 4)
         for t in range(PACK):
             steps[t]()
@@ -271,11 +294,13 @@ def tile_list_drum_level_median_kernel(
         def finish(g, h, between):
             between[0]()
             vote(g, h, 0, HB)
+            weave_h(g, h, 0, HB, nc.scalar.copy)
             between[1]()
             vote(g, h, HB, HB)
+            weave_h(g, h, HB, HB, nc.scalar.copy)
             between[2]()
-            quantise_h(g, h, 0, BANK)
             between[3]()
+            quantise_h(g, h, 0, BANK)
 
         finish(0, 0, [lambda t=t: cap(0, 1, t) for t in range(PACK)])
         finish(0, 1, [lambda t=t: low_high(1, 0, t) for t in range(PACK)])
@@ -295,12 +320,33 @@ def tile_list_drum_level_median_kernel(
                 low_high(1, 1, t + 1)
         steps[0]()
         steps[1]()
-        finish(1, 0, [lambda t=t: cap(1, 1, t) for t in range(PACK)])
-        scores(0, 0, BANK, "scalar_side")
-        tail = [(0, 256), (256, 128), (384, 128)]
-        vote(1, 1, *tail[0])
-        for k in range(len(tail)):
-            if k + 1 < len(tail):
-                vote(1, 1, *tail[k + 1])
-            quantise_h(1, 1, tail[k][0], tail[k][1])
-            scores(1, tail[k][0], tail[k][1], ["l3", "scalar_side"][k % 2])
+        QB = BANK // 4
+        banks = open_scores(0, 0, BANK, "scalar_side", 3)
+        cap(1, 1, 0, 0, HB)
+        vote(1, 0, 0, HB)
+        weave_h(1, 0, 0, HB, nc.scalar.copy)
+        cap(1, 1, 1, 0, HB)
+        vote(1, 0, HB, HB)
+        weave_h(1, 0, HB, HB, nc.scalar.copy)
+        cap(1, 1, 2, 0, HB)
+        cap(1, 1, 3, 0, HB)
+        cap(1, 1, 0, HB, HB)
+        vote(1, 1, 0, HB)
+        weave_h(1, 1, 0, HB, nc.scalar.copy)
+        quantise_h(1, 0, 0, BANK)
+        close_scores(0, 0, BANK, banks)
+        banks = open_scores(1, 0, HB, "scalar_side", 3)
+        for t in range(1, PACK):
+            cap(1, 1, t, HB, HB)
+        quantise_h(1, 1, 0, HB)
+        close_scores(1, 0, HB, banks)
+        banks_b = open_scores(1, HB, QB, "l3", 3)
+        banks_c = open_scores(1, HB + QB, QB, "scalar_side", 3)
+        vote(1, 1, HB, QB)
+        weave_h(1, 1, HB, QB, nc.scalar.copy)
+        vote(1, 1, HB + QB, QB)
+        weave_h(1, 1, HB + QB, QB, nc.vector.tensor_copy)
+        quantise_h(1, 1, HB, QB)
+        close_scores(1, HB, QB, banks_b)
+        quantise_h(1, 1, HB + QB, QB)
+        close_scores(1, HB + QB, QB, banks_c)

@@ -49,17 +49,15 @@ def tile_list_drum_level_median_kernel(
         xs_w = [held("xs_w%d" % a, [P, S], U32) for a in range(2)]
         xs_s = held("xs_s", [P, S], U8)
         bias_rows = held("bias_rows", [P, P], F32)
-        identity = held("identity", [P, P], F32)
         bias = held("bias", [P, 16], F32)
 
         nc.vector.memset(tab_s[:].bitcast(I32), 0)
         nc.vector.memset(w2_raw_s[:], 0)
         nc.vector.memset(xs_s[:].bitcast(I32), 0)
         nc.vector.memset(bias_rows[:], 0.0)
-        nc.vector.memset(identity[:], 0.0)
 
-        def load_weight(src, a, g):
-            raw = ring.tile([P, PACK, PASS], F32, name="w_raw", tag="w_raw", bufs=4, align_bytes=64)
+        def load_weight(src, a, g, tag="w_raw", bufs=4):
+            raw = ring.tile([P, PACK, PASS], F32, name="w_raw", tag=tag, bufs=bufs, align_bytes=64)
             rows = src[a * PASS : (a + 1) * PASS, g * PASS : (g + 1) * PASS]
             nc.sync.dma_start(out=raw[:], in_=rows.rearrange("(p j) c -> p j c", j=PACK))
             return raw
@@ -76,8 +74,14 @@ def tile_list_drum_level_median_kernel(
             nc.sync.dma_start(
                 out=w2_raw_s[32 * q : 32 * q + 4, :], in_=w2_scales[0, 4 * q : 4 * q + 4, :].bitcast(I32)
             )
-        make_identity(nc, identity[:], nomemset=True)
-        wx_raw = {(a, 0): load_weight(wx, a, 0) for a in range(2)}
+        wx_raw = {(0, 0): load_weight(wx, 0, 0, "then_identity", 1)}
+        wx_raw[(1, 0)] = load_weight(wx, 1, 0)
+        bx_by_slot = bx.rearrange("(g u t i) -> g t u i", g=GROUPS, t=PACK, i=4)
+        for g in range(GROUPS):
+            nc.sync.dma_start(
+                out=bias_rows[g * PACK : (g + 1) * PACK, :].rearrange("t (u i) -> t u i", i=4), in_=bx_by_slot[g]
+            )
+        nc.sync.dma_start(out=bias_rows[BO : BO + N_TILES, :], in_=bo.rearrange("(a p) -> a p", p=P))
         for a in range(2):
             nc.sync.dma_start(out=xs_w[a][:].bitcast(I32), in_=xs_words[a].rearrange("p c i -> p (c i)").bitcast(I32))
             for q in range(2 * a, 2 * a + 2):
@@ -85,12 +89,6 @@ def tile_list_drum_level_median_kernel(
                     out=xs_s[32 * q : 32 * q + 8, :].bitcast(I32), in_=xs_scales[:, 4 * q : 4 * q + 4, :].bitcast(I32)
                 )
         w1_raw[1] = load_weight(w1, 0, 1)
-        bx_by_slot = bx.rearrange("(g u t i) -> g t u i", g=GROUPS, t=PACK, i=4)
-        for g in range(GROUPS):
-            nc.sync.dma_start(
-                out=bias_rows[g * PACK : (g + 1) * PACK, :].rearrange("t (u i) -> t u i", i=4), in_=bx_by_slot[g]
-            )
-        nc.sync.dma_start(out=bias_rows[BO : BO + N_TILES, :], in_=bo.rearrange("(a p) -> a p", p=P))
         for a in range(2):
             wx_raw[(a, 1)] = load_weight(wx, a, 1)
         wo_raw = [held("wo_raw%d" % g, [P, PACK, N], F32) for g in range(GROUPS)]
@@ -123,9 +121,9 @@ def tile_list_drum_level_median_kernel(
             )
 
         def weave_weight(raw):
-            woven = ring.tile([P, PACK * PASS], BF16, name="woven", tag="woven", bufs=3, align_bytes=64)
-            dst = woven[:].rearrange("p (t u i j) -> p t u i j", t=PACK, i=4, j=PACK)
-            src = raw[:].rearrange("p j (u t i) -> p t u i j", t=PACK, i=4)
+            woven = ring.tile([P, PACK * PASS], BF16, name="woven", tag="woven", bufs=1, align_bytes=64)
+            dst = woven[:].rearrange("p (t u i j) -> p t u j i", t=PACK, i=4, j=PACK)
+            src = raw[:].rearrange("p j (u t i) -> p t u j i", t=PACK, i=4)
             for t in range(PACK):
                 nc.scalar.copy(out=dst[:, t], in_=src[:, t])
             return woven
@@ -147,7 +145,7 @@ def tile_list_drum_level_median_kernel(
             return (codes, scales), steps
 
         w1_q, wx_q = {}, {}
-        low, high, mid, voted, h_woven, h_q = {}, {}, {}, {}, {}, {}
+        low, high, mid, h_woven, h_q = {}, {}, {}, {}, {}
 
         def low_high(g, h, t):
             cols = slice(t * P, (t + 1) * P)
@@ -162,7 +160,7 @@ def tile_list_drum_level_median_kernel(
                 start=True,
                 stop=True,
             )
-            l2 = ring.tile([P, BANK], F32, name="l2", tag="l2", bufs=4)
+            l2 = ring.tile([P, BANK], F32, name="l2", tag="l2", bufs=6)
             nc.scalar.copy(out=l2[:], in_=l2_ps[:])
             l1_ps = psum.tile([P, BANK], F32, name="l1_ps", tag="l1", bufs=2)
             codes, scales = w1_q[g]
@@ -209,17 +207,13 @@ def tile_list_drum_level_median_kernel(
 
         def vote(g, h, c0, width):
             if c0 == 0:
-                voted[(g, h)] = ring.tile([P, PACK, BANK], BF16, name="voted", tag="voted", bufs=2)
                 h_woven[(g, h)] = ring.tile([P, PACK * BANK], BF16, name="h_woven", tag="h_woven", bufs=2, align_bytes=64)
-            toks = slice(c0, c0 + width)
+            walk = "p t (c i) -> p c t i"
             nc.vector.tensor_tensor(
-                out=voted[(g, h)][:, :, toks], in0=low[(g, h)][:, :, toks], in1=mid[(g, h)][:, :, toks], op=ALU.max
-            )
-
-        def weave_h(g, h, c0, width, copy):
-            copy(
-                out=h_woven[(g, h)][:, PACK * c0 : PACK * (c0 + width)].rearrange("p (j t) -> p j t", t=PACK),
-                in_=voted[(g, h)][:, :, c0 : c0 + width].rearrange("p t j -> p j t"),
+                out=h_woven[(g, h)][:, PACK * c0 : PACK * (c0 + width)].rearrange("p (c i t) -> p c t i", i=4, t=PACK),
+                in0=low[(g, h)][:, :, c0 : c0 + width].rearrange(walk, i=4),
+                in1=mid[(g, h)][:, :, c0 : c0 + width].rearrange(walk, i=4),
+                op=ALU.max,
             )
 
         def quantise_h(g, h, c0, width):
@@ -279,6 +273,8 @@ def tile_list_drum_level_median_kernel(
         wx_q[(1, 0)], steps1 = quantise("wxq10", weave_weight(wx_raw[(1, 0)]), [2048])
         low_high(0, 1, 2)
         steps1[0]()
+        identity = ring.tile([P, P], F32, name="identity", tag="then_identity", bufs=1, align_bytes=64)
+        make_identity(nc, identity[:])
         bias_ps = psum.tile([P, P], F32, name="bias_ps", tag="scalar_side", bufs=3)
         nc.tensor.transpose(bias_ps[:], bias_rows[:], identity[:])
         nc.scalar.copy(out=bias[:], in_=bias_ps[:, 0:16])
@@ -289,30 +285,28 @@ def tile_list_drum_level_median_kernel(
             cap(0, 0, t)
         steps[0]()
         wx_q[(0, 1)], steps0 = quantise("wxq01", weave_weight(wx_raw[(0, 1)]), [2048])
-        wx_q[(1, 1)], steps1 = quantise("wxq11", weave_weight(wx_raw[(1, 1)]), [2048])
 
         def finish(g, h, between):
             between[0]()
             vote(g, h, 0, HB)
-            weave_h(g, h, 0, HB, nc.scalar.copy)
             between[1]()
             vote(g, h, HB, HB)
-            weave_h(g, h, HB, HB, nc.scalar.copy)
             between[2]()
-            between[3]()
             quantise_h(g, h, 0, BANK)
+            between[3]()
 
         finish(0, 0, [lambda t=t: cap(0, 1, t) for t in range(PACK)])
-        finish(0, 1, [lambda t=t: low_high(1, 0, t) for t in range(PACK)])
         steps0[0]()
-        low_high(1, 1, 0)
+        wx_q[(1, 1)], steps1 = quantise("wxq11", weave_weight(wx_raw[(1, 1)]), [2048])
+        finish(0, 1, [lambda t=t: low_high(1, 0, t) for t in range(PACK)])
         steps1[0]()
-        wo_woven = held("wo_woven", [P, GROUPS * N * PACK], BF16)
+        low_high(1, 1, 0)
+        wo_woven = ring.tile([P, GROUPS * N * PACK], BF16, name="wo_woven", tag="woven", bufs=1, align_bytes=64)
         for g in range(GROUPS):
-            dst = wo_woven[:, g * N * PACK : (g + 1) * N * PACK].rearrange("p (n t) -> p n t", t=PACK)
-            src = wo_raw[g][:].rearrange("p t n -> p n t")
+            dst = wo_woven[:, g * N * PACK : (g + 1) * N * PACK].rearrange("p (c i t) -> p c t i", i=4, t=PACK)
+            src = wo_raw[g][:].rearrange("p t (c i) -> p c t i", i=4)
             for n in range(N_TILES):
-                nc.scalar.copy(out=dst[:, n * P : (n + 1) * P], in_=src[:, n * P : (n + 1) * P])
+                nc.scalar.copy(out=dst[:, n * 32 : (n + 1) * 32], in_=src[:, n * 32 : (n + 1) * 32])
         wo_q, steps = quantise("woq", wo_woven, [2048, 1024])
         for t in range(PACK):
             cap(1, 0, t)
@@ -324,28 +318,24 @@ def tile_list_drum_level_median_kernel(
         banks = open_scores(0, 0, BANK, "scalar_side", 3)
         cap(1, 1, 0, 0, HB)
         vote(1, 0, 0, HB)
-        weave_h(1, 0, 0, HB, nc.scalar.copy)
         cap(1, 1, 1, 0, HB)
         vote(1, 0, HB, HB)
-        weave_h(1, 0, HB, HB, nc.scalar.copy)
         cap(1, 1, 2, 0, HB)
+        quantise_h(1, 0, 0, BANK)
+        close_scores(0, 0, BANK, banks)
         cap(1, 1, 3, 0, HB)
         cap(1, 1, 0, HB, HB)
         vote(1, 1, 0, HB)
-        weave_h(1, 1, 0, HB, nc.scalar.copy)
-        quantise_h(1, 0, 0, BANK)
-        close_scores(0, 0, BANK, banks)
         banks = open_scores(1, 0, HB, "scalar_side", 3)
-        for t in range(1, PACK):
-            cap(1, 1, t, HB, HB)
+        cap(1, 1, 1, HB, HB)
         quantise_h(1, 1, 0, HB)
         close_scores(1, 0, HB, banks)
+        for t in range(2, PACK):
+            cap(1, 1, t, HB, HB)
         banks_b = open_scores(1, HB, QB, "l3", 3)
         banks_c = open_scores(1, HB + QB, QB, "scalar_side", 3)
         vote(1, 1, HB, QB)
-        weave_h(1, 1, HB, QB, nc.scalar.copy)
         vote(1, 1, HB + QB, QB)
-        weave_h(1, 1, HB + QB, QB, nc.vector.tensor_copy)
         quantise_h(1, 1, HB, QB)
         close_scores(1, HB, QB, banks_b)
         quantise_h(1, 1, HB + QB, QB)

@@ -19,12 +19,20 @@ IDENTITY = mybir.ActivationFunctionType.Identity
 
 P = 128
 PACK = 4
-PASS = 512
-BANK = 512
+RUN = 4
+PASS = P * PACK
+HALF = 512
+QUARTER = HALF // 2
+EIGHTH = HALF // 4
 GROUPS = H // PASS
-HALVES = S // BANK
 N_TILES = N // P
-BO = GROUPS * PACK
+QUADRANTS = 4
+BO_COLUMN = GROUPS * PACK
+BIAS_COLUMNS = BO_COLUMN + N_TILES
+
+SCALAR_BANKS = ("scalar_side", 3)
+L1_BANKS = ("l1", 2)
+L3_BANKS = ("l3", 3)
 
 
 def tile_list_drum_level_median_kernel(
@@ -39,17 +47,20 @@ def tile_list_drum_level_median_kernel(
         def held(name, shape, dtype):
             return keep.tile(shape, dtype, name=name, align_bytes=64)
 
+        def bank(name, width, banks):
+            return psum.tile([P, width], F32, name=name, tag=banks[0], bufs=banks[1])
+
         offsets = keep.tile([P, S // 16], U16, name="offsets")
         tab_w = held("tab_w", [P, T], U32)
         tab_s = held("tab_s", [P, T], U8)
         w2_raw_w = held("w2_raw_w", [P, H // 2], I32)
-        w2_raw_s = keep.tile([P, H // 4], I32, name="w2_raw_s", tag="scales_twice", align_bytes=64)
+        w2_raw_s = keep.tile([P, H // 4], I32, name="w2_raw_s", tag="then_v_s", align_bytes=64)
         w2_w = held("w2_w", [P, 2 * H], U8)
         w2_s = held("w2_s", [P, H], U8)
-        xs_w = [held("xs_w%d" % a, [P, S], U32) for a in range(2)]
+        xs_w = [held("xs_w%d" % a, [P, S], U32) for a in range(K2 // PASS)]
         xs_s = held("xs_s", [P, S], U8)
         bias_rows = held("bias_rows", [P, P], F32)
-        bias = held("bias", [P, 16], F32)
+        bias = held("bias", [P, BIAS_COLUMNS], F32)
 
         nc.vector.memset(tab_s[:].bitcast(I32), 0)
         nc.vector.memset(w2_raw_s[:], 0)
@@ -64,279 +75,282 @@ def tile_list_drum_level_median_kernel(
 
         nc.sync.dma_start(out=tab_w[:].bitcast(I32), in_=tab_words[0].rearrange("p t i -> p (t i)").bitcast(I32))
         nc.sync.dma_start(offsets[:], offs)
-        for q in range(4):
+        for q in range(QUADRANTS):
             nc.sync.dma_start(
                 out=tab_s[32 * q : 32 * q + 4, :].bitcast(I32), in_=tab_scales[0, 4 * q : 4 * q + 4, :].bitcast(I32)
             )
         w1_raw = {0: load_weight(w1, 0, 0)}
         nc.sync.dma_start(out=w2_raw_w[:], in_=w2_words[0].bitcast(I32))
-        for q in range(4):
-            nc.sync.dma_start(
-                out=w2_raw_s[32 * q : 32 * q + 4, :], in_=w2_scales[0, 4 * q : 4 * q + 4, :].bitcast(I32)
-            )
+        for q in range(QUADRANTS):
+            nc.sync.dma_start(out=w2_raw_s[32 * q : 32 * q + 4, :], in_=w2_scales[0, 4 * q : 4 * q + 4, :].bitcast(I32))
         wx_raw = {(0, 0): load_weight(wx, 0, 0, "then_identity", 1)}
         wx_raw[(1, 0)] = load_weight(wx, 1, 0)
-        bx_by_slot = bx.rearrange("(g u t i) -> g t u i", g=GROUPS, t=PACK, i=4)
+        bx_by_slot = bx.rearrange("(g u t i) -> g t u i", g=GROUPS, t=PACK, i=RUN)
         for g in range(GROUPS):
             nc.sync.dma_start(
-                out=bias_rows[g * PACK : (g + 1) * PACK, :].rearrange("t (u i) -> t u i", i=4), in_=bx_by_slot[g]
+                out=bias_rows[g * PACK : (g + 1) * PACK, :].rearrange("t (u i) -> t u i", i=RUN), in_=bx_by_slot[g]
             )
-        nc.sync.dma_start(out=bias_rows[BO : BO + N_TILES, :], in_=bo.rearrange("(a p) -> a p", p=P))
-        for a in range(2):
+        nc.sync.dma_start(out=bias_rows[BO_COLUMN:BIAS_COLUMNS, :], in_=bo.rearrange("(a p) -> a p", p=P))
+        for a in range(K2 // PASS):
             nc.sync.dma_start(out=xs_w[a][:].bitcast(I32), in_=xs_words[a].rearrange("p c i -> p (c i)").bitcast(I32))
             for q in range(2 * a, 2 * a + 2):
                 nc.sync.dma_start(
                     out=xs_s[32 * q : 32 * q + 8, :].bitcast(I32), in_=xs_scales[:, 4 * q : 4 * q + 4, :].bitcast(I32)
                 )
         w1_raw[1] = load_weight(w1, 0, 1)
-        for a in range(2):
+        for a in range(K2 // PASS):
             wx_raw[(a, 1)] = load_weight(wx, a, 1)
         wo_raw = [held("wo_raw%d" % g, [P, PACK, N], F32) for g in range(GROUPS)]
-        wo_by_slot = wo.rearrange("(g u t i) n -> g t u i n", g=GROUPS, t=PACK, i=4)
+        wo_by_slot = wo.rearrange("(g u t i) n -> g t u i n", g=GROUPS, t=PACK, i=RUN)
         for g in range(GROUPS):
             for t in range(PACK):
                 nc.sync.dma_start(out=wo_raw[g][:, t, :], in_=wo_by_slot[g, t])
 
         v_w, v_s = {}, {}
 
-        def picks(h):
-            return offsets[:, h * (BANK // 16) : (h + 1) * (BANK // 16)]
+        def picks(half):
+            return offsets[:, half * (HALF // 16) : (half + 1) * (HALF // 16)]
 
-        def gather_words(h):
-            v_w[h] = held("v_w%d" % h, [P, BANK], U32)
-            nc.vector.tensor_copy(v_w[h][:], tab_w[:].indirect(picks(h)))
+        def gather_words(half):
+            v_w[half] = held("v_w%d" % half, [P, HALF], U32)
+            nc.vector.tensor_copy(v_w[half][:], tab_w[:].indirect(picks(half)))
 
-        def gather_scales(h, tag):
-            v_s[h] = keep.tile([P, BANK], U8, name="v_s", tag=tag, align_bytes=64)
-            nc.vector.tensor_copy(v_s[h][:], tab_s[:].indirect(picks(h)))
+        def gather_scales(half, tag):
+            v_s[half] = keep.tile([P, HALF], U8, name="v_s", tag=tag, align_bytes=64)
+            nc.vector.tensor_copy(v_s[half][:], tab_s[:].indirect(picks(half)))
 
-        def deal_w2():
+        def order_w2_words(g):
             nc.vector.tensor_copy(
-                out=w2_w[:].bitcast(I32).rearrange("p (g t u e) -> p g t u e", g=GROUPS, t=PACK, e=2),
-                in_=w2_raw_w[:].rearrange("p (g u t e) -> p g t u e", g=GROUPS, t=PACK, e=2),
+                out=w2_w[:].bitcast(I32).rearrange("p (g t u e) -> p g t u e", g=GROUPS, t=PACK, e=2)[:, g],
+                in_=w2_raw_w[:].rearrange("p (g u t e) -> p g t u e", g=GROUPS, t=PACK, e=2)[:, g],
             )
+
+        def order_w2_scales():
             nc.vector.tensor_copy(
                 out=w2_s[:].bitcast(I32).rearrange("p (g t u) -> p g t u", g=GROUPS, t=PACK),
                 in_=w2_raw_s[:].rearrange("p (g u t) -> p g t u", g=GROUPS, t=PACK),
             )
 
+        def woven_tile(width):
+            return ring.tile([P, width], BF16, name="woven", tag="woven", bufs=1, align_bytes=64)
+
         def weave_weight(raw):
-            woven = ring.tile([P, PACK * PASS], BF16, name="woven", tag="woven", bufs=1, align_bytes=64)
-            dst = woven[:].rearrange("p (t u i j) -> p t u j i", t=PACK, i=4, j=PACK)
-            src = raw[:].rearrange("p j (u t i) -> p t u j i", t=PACK, i=4)
+            woven = woven_tile(PACK * PASS)
+            dst = woven[:].rearrange("p (t u i j) -> p t u j i", t=PACK, i=RUN, j=PACK)
+            src = raw[:].rearrange("p j (u t i) -> p t u j i", t=PACK, i=RUN)
             for t in range(PACK):
                 nc.scalar.copy(out=dst[:, t], in_=src[:, t])
             return woven
 
-        def quantise(name, woven, pieces):
-            cols = sum(pieces) // PACK
-            codes = held(name + "_w", [P, cols], U32)
-            scales = held(name + "_s", [P, cols], U8)
-            at = 0
-            steps = []
-            for width in pieces:
-                c = slice(at // PACK, (at + width) // PACK)
-                steps.append(
-                    lambda c=c, at=at, width=width: nc.vector.quantize_mx(
-                        out=codes[:, c].bitcast(FP8X4), scales=scales[:, c], in_=woven[:, at : at + width]
-                    )
-                )
-                at = at + width
-            return (codes, scales), steps
+        def weave_wo():
+            woven = woven_tile(GROUPS * N * PACK)
+            runs = P // RUN
+            for g in range(GROUPS):
+                dst = woven[:, g * N * PACK : (g + 1) * N * PACK].rearrange("p (c i t) -> p c t i", i=RUN, t=PACK)
+                src = wo_raw[g][:].rearrange("p t (c i) -> p c t i", i=RUN)
+                for n in range(N_TILES):
+                    nc.scalar.copy(out=dst[:, n * runs : (n + 1) * runs], in_=src[:, n * runs : (n + 1) * runs])
+            return woven
 
-        w1_q, wx_q = {}, {}
-        low, high, mid, h_woven, h_q = {}, {}, {}, {}, {}
+        def mx_tiles(name, columns):
+            return held(name + "_w", [P, columns], U32), held(name + "_s", [P, columns], U8)
 
-        def low_high(g, h, t):
-            cols = slice(t * P, (t + 1) * P)
+        def quantise(operand, woven, c0, columns):
+            words, scales = operand
+            nc.vector.quantize_mx(
+                out=words[:, c0 : c0 + columns].bitcast(FP8X4),
+                scales=scales[:, c0 : c0 + columns],
+                in_=woven[:, PACK * c0 : PACK * (c0 + columns)],
+            )
+
+        w1_q = [mx_tiles("w1q%d" % g, PASS) for g in range(GROUPS)]
+        wx_q = {(a, g): mx_tiles("wxq%d%d" % (a, g), PASS) for a in range(K2 // PASS) for g in range(GROUPS)}
+        wo_q = mx_tiles("woq", GROUPS * N)
+        h_q = {(g, half): mx_tiles("hq%d%d" % (g, half), HALF) for g in range(GROUPS) for half in range(S // HALF)}
+        low, high, capped, h_woven = {}, {}, {}, {}
+
+        def low_high(g, half, t):
             c0 = g * PASS + t * P
-            l2_ps = psum.tile([P, BANK], F32, name="l2_ps", tag="scalar_side", bufs=3)
+            l2_ps = bank("l2_ps", HALF, SCALAR_BANKS)
             nc.tensor.matmul_mx(
                 out=l2_ps[:],
                 lhsT=w2_w[:, 2 * c0 : 2 * (c0 + P)].bitcast(FP4X4),
                 lhsT_scale=w2_s[:, c0 : c0 + P],
-                rhs=v_w[h][:].bitcast(FP8X4),
-                rhs_scale=v_s[h][:],
+                rhs=v_w[half][:].bitcast(FP8X4),
+                rhs_scale=v_s[half][:],
                 start=True,
                 stop=True,
             )
-            l2 = ring.tile([P, BANK], F32, name="l2", tag="l2", bufs=6)
+            l2 = ring.tile([P, HALF], F32, name="l2", tag="l2", bufs=6)
             nc.scalar.copy(out=l2[:], in_=l2_ps[:])
-            l1_ps = psum.tile([P, BANK], F32, name="l1_ps", tag="l1", bufs=2)
-            codes, scales = w1_q[g]
+            l1_ps = bank("l1_ps", HALF, L1_BANKS)
+            words, scales = w1_q[g]
             nc.tensor.matmul_mx(
                 out=l1_ps[:],
-                lhsT=codes[:, cols].bitcast(FP8X4),
-                lhsT_scale=scales[:, cols],
-                rhs=v_w[h][:].bitcast(FP8X4),
-                rhs_scale=v_s[h][:],
+                lhsT=words[:, t * P : (t + 1) * P].bitcast(FP8X4),
+                lhsT_scale=scales[:, t * P : (t + 1) * P],
+                rhs=v_w[half][:].bitcast(FP8X4),
+                rhs_scale=v_s[half][:],
                 start=True,
                 stop=True,
             )
             if t == 0:
-                low[(g, h)] = ring.tile([P, PACK, BANK], F32, name="low", tag="low", bufs=3)
-            high[(g, h, t)] = ring.tile([P, BANK], F32, name="high", tag="high", bufs=8)
-            nc.vector.tensor_tensor(out=low[(g, h)][:, t, :], in0=l1_ps[:], in1=l2[:], op=ALU.min)
-            nc.vector.tensor_tensor(out=high[(g, h, t)][:], in0=l1_ps[:], in1=l2[:], op=ALU.max)
+                low[(g, half)] = ring.tile([P, PACK, HALF], F32, name="low", tag="low", bufs=3)
+            high[(g, half, t)] = ring.tile([P, HALF], F32, name="high", tag="high", bufs=8)
+            nc.vector.tensor_tensor(out=low[(g, half)][:, t, :], in0=l1_ps[:], in1=l2[:], op=ALU.min)
+            nc.vector.tensor_tensor(out=high[(g, half, t)][:], in0=l1_ps[:], in1=l2[:], op=ALU.max)
 
-        def cap(g, h, t, c0=0, width=BANK):
-            cols = slice(t * P, (t + 1) * P)
-            toks = slice(h * BANK + c0, h * BANK + c0 + width)
-            l3_ps = psum.tile([P, width], F32, name="l3_ps", tag="l3", bufs=3)
-            for a in range(2):
-                codes, scales = wx_q[(a, g)]
+        def cap(g, half, t, c0=0, width=HALF):
+            entries = slice(half * HALF + c0, half * HALF + c0 + width)
+            l3_ps = bank("l3_ps", width, L3_BANKS)
+            for a in range(K2 // PASS):
+                words, scales = wx_q[(a, g)]
                 nc.tensor.matmul_mx(
                     out=l3_ps[:],
-                    lhsT=codes[:, cols].bitcast(FP8X4),
-                    lhsT_scale=scales[:, cols],
-                    rhs=xs_w[a][:, toks].bitcast(FP8X4),
-                    rhs_scale=xs_s[4 * a : P, toks],
+                    lhsT=words[:, t * P : (t + 1) * P].bitcast(FP8X4),
+                    lhsT_scale=scales[:, t * P : (t + 1) * P],
+                    rhs=xs_w[a][:, entries].bitcast(FP8X4),
+                    rhs_scale=xs_s[4 * a : P, entries],
                     start=(a == 0),
-                    stop=(a == 1),
+                    stop=(a == K2 // PASS - 1),
                 )
             if t == 0 and c0 == 0:
-                mid[(g, h)] = ring.tile([P, PACK, BANK], F32, name="mid", tag="mid", bufs=2)
+                capped[(g, half)] = ring.tile([P, PACK, HALF], F32, name="capped", tag="capped", bufs=2)
             nc.vector.scalar_tensor_tensor(
-                out=mid[(g, h)][:, t, c0 : c0 + width],
+                out=capped[(g, half)][:, t, c0 : c0 + width],
                 in0=l3_ps[:],
                 scalar=bias[:, g * PACK + t : g * PACK + t + 1],
-                in1=high[(g, h, t)][:, c0 : c0 + width],
+                in1=high[(g, half, t)][:, c0 : c0 + width],
                 op0=ALU.add,
                 op1=ALU.min,
             )
 
-        def vote(g, h, c0, width):
+        def vote(g, half, c0, width):
             if c0 == 0:
-                h_woven[(g, h)] = ring.tile([P, PACK * BANK], BF16, name="h_woven", tag="h_woven", bufs=2, align_bytes=64)
-            walk = "p t (c i) -> p c t i"
+                h_woven[(g, half)] = ring.tile(
+                    [P, PACK * HALF], BF16, name="h_woven", tag="h_woven", bufs=2, align_bytes=64
+                )
+            by_runs = "p t (c i) -> p c t i"
             nc.vector.tensor_tensor(
-                out=h_woven[(g, h)][:, PACK * c0 : PACK * (c0 + width)].rearrange("p (c i t) -> p c t i", i=4, t=PACK),
-                in0=low[(g, h)][:, :, c0 : c0 + width].rearrange(walk, i=4),
-                in1=mid[(g, h)][:, :, c0 : c0 + width].rearrange(walk, i=4),
+                out=h_woven[(g, half)][:, PACK * c0 : PACK * (c0 + width)].rearrange(
+                    "p (c i t) -> p c t i", i=RUN, t=PACK
+                ),
+                in0=low[(g, half)][:, :, c0 : c0 + width].rearrange(by_runs, i=RUN),
+                in1=capped[(g, half)][:, :, c0 : c0 + width].rearrange(by_runs, i=RUN),
                 op=ALU.max,
             )
 
-        def quantise_h(g, h, c0, width):
-            if (g, h) not in h_q:
-                h_q[(g, h)] = (held("h_w%d%d" % (g, h), [P, BANK], U32), held("h_s%d%d" % (g, h), [P, BANK], U8))
-            codes, scales = h_q[(g, h)]
-            nc.vector.quantize_mx(
-                out=codes[:, c0 : c0 + width].bitcast(FP8X4), scales=scales[:, c0 : c0 + width], in_=h_woven[(g, h)][:, PACK * c0 : PACK * (c0 + width)]
-            )
+        def quantise_h(g, half, c0, width):
+            quantise(h_q[(g, half)], h_woven[(g, half)], c0, width)
 
-        def score_pass(y_ps, n, g, h, c0, width):
-            codes, scales = wo_q
-            cols = slice(g * N + n * P, g * N + (n + 1) * P)
+        def vote_half(g, half, between):
+            between(0)
+            vote(g, half, 0, QUARTER)
+            between(1)
+            vote(g, half, QUARTER, QUARTER)
+            between(2)
+            quantise_h(g, half, 0, HALF)
+            between(3)
+
+        def score_pass(y_ps, n, g, half, c0, width):
+            columns = slice(g * N + n * P, g * N + (n + 1) * P)
             nc.tensor.matmul_mx(
                 out=y_ps[:],
-                lhsT=codes[:, cols].bitcast(FP8X4),
-                lhsT_scale=scales[:, cols],
-                rhs=h_q[(g, h)][0][:, c0 : c0 + width].bitcast(FP8X4),
-                rhs_scale=h_q[(g, h)][1][:, c0 : c0 + width],
+                lhsT=wo_q[0][:, columns].bitcast(FP8X4),
+                lhsT_scale=wo_q[1][:, columns],
+                rhs=h_q[(g, half)][0][:, c0 : c0 + width].bitcast(FP8X4),
+                rhs_scale=h_q[(g, half)][1][:, c0 : c0 + width],
                 start=(g == 0),
                 stop=(g == GROUPS - 1),
             )
 
-        def open_scores(h, c0, width, tag, bufs):
-            banks = []
+        def open_scores(half, c0, width, banks):
+            sums = []
             for n in range(N_TILES):
-                y_ps = psum.tile([P, width], F32, name="y_ps", tag=tag, bufs=bufs)
-                score_pass(y_ps, n, 0, h, c0, width)
-                banks.append(y_ps)
-            return banks
+                y_ps = bank("y_ps", width, banks)
+                score_pass(y_ps, n, 0, half, c0, width)
+                sums.append(y_ps)
+            return sums
 
-        def close_scores(h, c0, width, banks):
-            staged = held("staged%d_%d" % (h, c0), [P, N_TILES, width], F32)
+        def close_scores(half, c0, width, sums):
+            staged = held("staged%d_%d" % (half, c0), [P, N_TILES, width], F32)
             for n in range(N_TILES):
-                score_pass(banks[n], n, 1, h, c0, width)
-                nc.scalar.activation(out=staged[:, n, :], in_=banks[n][:], func=IDENTITY, bias=bias[:, BO + n : BO + n + 1])
-            j0 = h * BANK + c0
+                score_pass(sums[n], n, 1, half, c0, width)
+                nc.scalar.activation(
+                    out=staged[:, n, :], in_=sums[n][:], func=IDENTITY, bias=bias[:, BO_COLUMN + n : BO_COLUMN + n + 1]
+                )
+            j0 = half * HALF + c0
             nc.sync.dma_start(out=out[:, j0 : j0 + width].rearrange("(a p) j -> p a j", p=P), in_=staged[:])
-
-        HB = BANK // 2
 
         gather_words(0)
         gather_scales(0, "v_s0")
         gather_words(1)
-        deal_w2()
-        gather_scales(1, "scales_twice")
-        w1_q[0], steps = quantise("w1q0", weave_weight(w1_raw[0]), [512] * 4)
+        order_w2_words(0)
+        order_w2_scales()
+        gather_scales(1, "then_v_s")
+        woven = weave_weight(w1_raw[0])
         for t in range(PACK):
-            steps[t]()
+            quantise(w1_q[0], woven, t * P, P)
             if t > 0:
                 low_high(0, 0, t - 1)
-        low_high(0, 0, 3)
-        wx_q[(0, 0)], steps0 = quantise("wxq00", weave_weight(wx_raw[(0, 0)]), [2048])
+        low_high(0, 0, PACK - 1)
+        order_w2_words(1)
+        woven = weave_weight(wx_raw[(0, 0)])
         low_high(0, 1, 0)
-        steps0[0]()
+        quantise(wx_q[(0, 0)], woven, 0, PASS)
         low_high(0, 1, 1)
-        wx_q[(1, 0)], steps1 = quantise("wxq10", weave_weight(wx_raw[(1, 0)]), [2048])
+        woven = weave_weight(wx_raw[(1, 0)])
         low_high(0, 1, 2)
-        steps1[0]()
+        quantise(wx_q[(1, 0)], woven, 0, PASS)
+
         identity = ring.tile([P, P], F32, name="identity", tag="then_identity", bufs=1, align_bytes=64)
         make_identity(nc, identity[:])
-        bias_ps = psum.tile([P, P], F32, name="bias_ps", tag="scalar_side", bufs=3)
+        bias_ps = bank("bias_ps", P, SCALAR_BANKS)
         nc.tensor.transpose(bias_ps[:], bias_rows[:], identity[:])
-        nc.scalar.copy(out=bias[:], in_=bias_ps[:, 0:16])
+        nc.scalar.copy(out=bias[:], in_=bias_ps[:, 0:BIAS_COLUMNS])
         low_high(0, 1, 3)
 
-        w1_q[1], steps = quantise("w1q1", weave_weight(w1_raw[1]), [2048])
+        woven = weave_weight(w1_raw[1])
         for t in range(PACK):
             cap(0, 0, t)
-        steps[0]()
-        wx_q[(0, 1)], steps0 = quantise("wxq01", weave_weight(wx_raw[(0, 1)]), [2048])
+        quantise(w1_q[1], woven, 0, PASS)
+        woven = weave_weight(wx_raw[(0, 1)])
+        vote_half(0, 0, lambda t: cap(0, 1, t))
+        quantise(wx_q[(0, 1)], woven, 0, PASS)
+        woven = weave_weight(wx_raw[(1, 1)])
+        vote_half(0, 1, lambda t: low_high(1, 0, t))
+        quantise(wx_q[(1, 1)], woven, 0, PASS)
 
-        def finish(g, h, between):
-            between[0]()
-            vote(g, h, 0, HB)
-            between[1]()
-            vote(g, h, HB, HB)
-            between[2]()
-            quantise_h(g, h, 0, BANK)
-            between[3]()
-
-        finish(0, 0, [lambda t=t: cap(0, 1, t) for t in range(PACK)])
-        steps0[0]()
-        wx_q[(1, 1)], steps1 = quantise("wxq11", weave_weight(wx_raw[(1, 1)]), [2048])
-        finish(0, 1, [lambda t=t: low_high(1, 0, t) for t in range(PACK)])
-        steps1[0]()
         low_high(1, 1, 0)
-        wo_woven = ring.tile([P, GROUPS * N * PACK], BF16, name="wo_woven", tag="woven", bufs=1, align_bytes=64)
-        for g in range(GROUPS):
-            dst = wo_woven[:, g * N * PACK : (g + 1) * N * PACK].rearrange("p (c i t) -> p c t i", i=4, t=PACK)
-            src = wo_raw[g][:].rearrange("p t (c i) -> p c t i", i=4)
-            for n in range(N_TILES):
-                nc.scalar.copy(out=dst[:, n * 32 : (n + 1) * 32], in_=src[:, n * 32 : (n + 1) * 32])
-        wo_q, steps = quantise("woq", wo_woven, [2048, 1024])
+        woven = weave_wo()
         for t in range(PACK):
             cap(1, 0, t)
-            if t < PACK - 1:
+            if t + 1 < PACK:
                 low_high(1, 1, t + 1)
-        steps[0]()
-        steps[1]()
-        QB = BANK // 4
-        banks = open_scores(0, 0, BANK, "scalar_side", 3)
-        cap(1, 1, 0, 0, HB)
-        vote(1, 0, 0, HB)
-        cap(1, 1, 1, 0, HB)
-        vote(1, 0, HB, HB)
-        cap(1, 1, 2, 0, HB)
-        quantise_h(1, 0, 0, BANK)
-        close_scores(0, 0, BANK, banks)
-        cap(1, 1, 3, 0, HB)
-        cap(1, 1, 0, HB, HB)
-        vote(1, 1, 0, HB)
-        banks = open_scores(1, 0, HB, "scalar_side", 3)
-        cap(1, 1, 1, HB, HB)
-        quantise_h(1, 1, 0, HB)
-        close_scores(1, 0, HB, banks)
-        for t in range(2, PACK):
-            cap(1, 1, t, HB, HB)
-        banks_b = open_scores(1, HB, QB, "l3", 3)
-        banks_c = open_scores(1, HB + QB, QB, "scalar_side", 3)
-        vote(1, 1, HB, QB)
-        vote(1, 1, HB + QB, QB)
-        quantise_h(1, 1, HB, QB)
-        close_scores(1, HB, QB, banks_b)
-        quantise_h(1, 1, HB + QB, QB)
-        close_scores(1, HB + QB, QB, banks_c)
+        quantise(wo_q, woven, 0, PASS)
+        quantise(wo_q, woven, PASS, GROUPS * N - PASS)
+
+        sums = open_scores(0, 0, HALF, SCALAR_BANKS)
+        cap(1, 1, 0, 0, QUARTER)
+        vote(1, 0, 0, QUARTER)
+        cap(1, 1, 1, 0, QUARTER)
+        vote(1, 0, QUARTER, QUARTER)
+        cap(1, 1, 2, 0, QUARTER)
+        quantise_h(1, 0, 0, HALF)
+        close_scores(0, 0, HALF, sums)
+        cap(1, 1, 3, 0, QUARTER)
+        cap(1, 1, 0, QUARTER, QUARTER)
+        vote(1, 1, 0, QUARTER)
+        sums = open_scores(1, 0, QUARTER, SCALAR_BANKS)
+        cap(1, 1, 1, QUARTER, QUARTER)
+        quantise_h(1, 1, 0, QUARTER)
+        close_scores(1, 0, QUARTER, sums)
+        cap(1, 1, 2, QUARTER, QUARTER)
+        cap(1, 1, 3, QUARTER, QUARTER)
+        last_pieces = [(QUARTER, L3_BANKS), (QUARTER + EIGHTH, SCALAR_BANKS)]
+        last_sums = [open_scores(1, c0, EIGHTH, banks) for c0, banks in last_pieces]
+        for c0, banks in last_pieces:
+            vote(1, 1, c0, EIGHTH)
+        for (c0, banks), sums in zip(last_pieces, last_sums):
+            quantise_h(1, 1, c0, EIGHTH)
+            close_scores(1, c0, EIGHTH, sums)

from contextlib import ExitStack

import concourse.mybir as mybir
from concourse.masks import make_identity

K, K2, H, N, T, S = 512, 1024, 1024, 384, 2048, 1024
FLOPS = 2 * S * H * (K + K + K2 + N)

F32 = mybir.dt.float32
BF16 = mybir.dt.bfloat16
I32 = mybir.dt.int32
U32 = mybir.dt.uint32
U16 = mybir.dt.uint16
U8 = mybir.dt.uint8
FP8X4 = mybir.dt.float8_e4m3fn_x4
FP4X4 = mybir.dt.float4_e2m1fn_x4
ALU = mybir.AluOpType
IDENTITY = mybir.ActivationFunctionType.Identity

P = 128
PACK = 4
RUN = 4
PASS = P * PACK
HALF = 512
QUARTER = HALF // 2
EIGHTH = HALF // 4
GROUPS = H // PASS
N_TILES = N // P
QUADRANTS = 4
BO_COLUMN = GROUPS * PACK
BIAS_COLUMNS = BO_COLUMN + N_TILES

SCALAR_BANKS = ("scalar_side", 3)
L1_BANKS = ("l1", 2)
L3_BANKS = ("l3", 3)


def tile_list_drum_level_median_kernel(
    tc, tab_words, tab_scales, offs, xs_words, xs_scales, w1, w2_words, w2_scales, wx, bx, wo, bo, out
):
    nc = tc.nc
    with ExitStack() as ctx:
        keep = ctx.enter_context(tc.tile_pool(name="keep", bufs=1))
        ring = ctx.enter_context(tc.tile_pool(name="ring", bufs=2))
        psum = ctx.enter_context(tc.psum_pool(name="psum", bufs=2))

        def held(name, shape, dtype):
            return keep.tile(shape, dtype, name=name, align_bytes=64)

        def bank(name, width, banks):
            return psum.tile([P, width], F32, name=name, tag=banks[0], bufs=banks[1])

        offsets = keep.tile([P, S // 16], U16, name="offsets")
        tab_w = held("tab_w", [P, T], U32)
        tab_s = held("tab_s", [P, T], U8)
        w2_raw_w = held("w2_raw_w", [P, H // 2], I32)
        w2_raw_s = keep.tile([P, H // 4], I32, name="w2_raw_s", tag="then_v_s", align_bytes=64)
        w2_w = held("w2_w", [P, 2 * H], U8)
        w2_s = held("w2_s", [P, H], U8)
        xs_w = [held("xs_w%d" % a, [P, S], U32) for a in range(K2 // PASS)]
        xs_s = held("xs_s", [P, S], U8)
        bias_rows = held("bias_rows", [P, P], F32)
        bias = held("bias", [P, BIAS_COLUMNS], F32)

        nc.vector.memset(tab_s[:].bitcast(I32), 0)
        nc.vector.memset(w2_raw_s[:], 0)
        nc.vector.memset(xs_s[:].bitcast(I32), 0)
        nc.vector.memset(bias_rows[:], 0.0)

        def load_weight(src, a, g, tag="w_raw", bufs=4):
            raw = ring.tile([P, PACK, PASS], F32, name="w_raw", tag=tag, bufs=bufs, align_bytes=64)
            rows = src[a * PASS : (a + 1) * PASS, g * PASS : (g + 1) * PASS]
            nc.sync.dma_start(out=raw[:], in_=rows.rearrange("(p j) c -> p j c", j=PACK))
            return raw

        nc.sync.dma_start(out=tab_w[:].bitcast(I32), in_=tab_words[0].rearrange("p t i -> p (t i)").bitcast(I32))
        nc.sync.dma_start(offsets[:], offs)
        for q in range(QUADRANTS):
            nc.sync.dma_start(
                out=tab_s[32 * q : 32 * q + 4, :].bitcast(I32), in_=tab_scales[0, 4 * q : 4 * q + 4, :].bitcast(I32)
            )
        w1_raw = {0: load_weight(w1, 0, 0)}
        nc.sync.dma_start(out=w2_raw_w[:], in_=w2_words[0].bitcast(I32))
        for q in range(QUADRANTS):
            nc.sync.dma_start(out=w2_raw_s[32 * q : 32 * q + 4, :], in_=w2_scales[0, 4 * q : 4 * q + 4, :].bitcast(I32))
        wx_raw = {(0, 0): load_weight(wx, 0, 0, "then_identity", 1)}
        wx_raw[(1, 0)] = load_weight(wx, 1, 0)
        bx_by_slot = bx.rearrange("(g u t i) -> g t u i", g=GROUPS, t=PACK, i=RUN)
        for g in range(GROUPS):
            nc.sync.dma_start(
                out=bias_rows[g * PACK : (g + 1) * PACK, :].rearrange("t (u i) -> t u i", i=RUN), in_=bx_by_slot[g]
            )
        nc.sync.dma_start(out=bias_rows[BO_COLUMN:BIAS_COLUMNS, :], in_=bo.rearrange("(a p) -> a p", p=P))
        for a in range(K2 // PASS):
            nc.sync.dma_start(out=xs_w[a][:].bitcast(I32), in_=xs_words[a].rearrange("p c i -> p (c i)").bitcast(I32))
            for q in range(2 * a, 2 * a + 2):
                nc.sync.dma_start(
                    out=xs_s[32 * q : 32 * q + 8, :].bitcast(I32), in_=xs_scales[:, 4 * q : 4 * q + 4, :].bitcast(I32)
                )
        w1_raw[1] = load_weight(w1, 0, 1)
        for a in range(K2 // PASS):
            wx_raw[(a, 1)] = load_weight(wx, a, 1)
        wo_raw = [held("wo_raw%d" % g, [P, PACK, N], F32) for g in range(GROUPS)]
        wo_by_slot = wo.rearrange("(g u t i) n -> g t u i n", g=GROUPS, t=PACK, i=RUN)
        for g in range(GROUPS):
            for t in range(PACK):
                nc.sync.dma_start(out=wo_raw[g][:, t, :], in_=wo_by_slot[g, t])

        v_w, v_s = {}, {}

        def picks(half):
            return offsets[:, half * (HALF // 16) : (half + 1) * (HALF // 16)]

        def gather_words(half):
            v_w[half] = held("v_w%d" % half, [P, HALF], U32)
            nc.vector.tensor_copy(v_w[half][:], tab_w[:].indirect(picks(half)))

        def gather_scales(half, tag):
            v_s[half] = keep.tile([P, HALF], U8, name="v_s", tag=tag, align_bytes=64)
            nc.vector.tensor_copy(v_s[half][:], tab_s[:].indirect(picks(half)))

        def order_w2_words(g):
            nc.vector.tensor_copy(
                out=w2_w[:].bitcast(I32).rearrange("p (g t u e) -> p g t u e", g=GROUPS, t=PACK, e=2)[:, g],
                in_=w2_raw_w[:].rearrange("p (g u t e) -> p g t u e", g=GROUPS, t=PACK, e=2)[:, g],
            )

        def order_w2_scales():
            nc.vector.tensor_copy(
                out=w2_s[:].bitcast(I32).rearrange("p (g t u) -> p g t u", g=GROUPS, t=PACK),
                in_=w2_raw_s[:].rearrange("p (g u t) -> p g t u", g=GROUPS, t=PACK),
            )

        def woven_tile(width):
            return ring.tile([P, width], BF16, name="woven", tag="woven", bufs=1, align_bytes=64)

        def weave_weight(raw):
            woven = woven_tile(PACK * PASS)
            dst = woven[:].rearrange("p (t u i j) -> p t u j i", t=PACK, i=RUN, j=PACK)
            src = raw[:].rearrange("p j (u t i) -> p t u j i", t=PACK, i=RUN)
            for t in range(PACK):
                nc.scalar.copy(out=dst[:, t], in_=src[:, t])
            return woven

        def weave_wo():
            woven = woven_tile(GROUPS * N * PACK)
            runs = P // RUN
            for g in range(GROUPS):
                dst = woven[:, g * N * PACK : (g + 1) * N * PACK].rearrange("p (c i t) -> p c t i", i=RUN, t=PACK)
                src = wo_raw[g][:].rearrange("p t (c i) -> p c t i", i=RUN)
                for n in range(N_TILES):
                    nc.scalar.copy(out=dst[:, n * runs : (n + 1) * runs], in_=src[:, n * runs : (n + 1) * runs])
            return woven

        def mx_tiles(name, columns):
            return held(name + "_w", [P, columns], U32), held(name + "_s", [P, columns], U8)

        def quantise(operand, woven, c0, columns):
            words, scales = operand
            nc.vector.quantize_mx(
                out=words[:, c0 : c0 + columns].bitcast(FP8X4),
                scales=scales[:, c0 : c0 + columns],
                in_=woven[:, PACK * c0 : PACK * (c0 + columns)],
            )

        w1_q = [mx_tiles("w1q%d" % g, PASS) for g in range(GROUPS)]
        wx_q = {(a, g): mx_tiles("wxq%d%d" % (a, g), PASS) for a in range(K2 // PASS) for g in range(GROUPS)}
        wo_q = mx_tiles("woq", GROUPS * N)
        h_q = {(g, half): mx_tiles("hq%d%d" % (g, half), HALF) for g in range(GROUPS) for half in range(S // HALF)}
        low, high, capped, h_woven = {}, {}, {}, {}

        def low_high(g, half, t):
            c0 = g * PASS + t * P
            l2_ps = bank("l2_ps", HALF, SCALAR_BANKS)
            nc.tensor.matmul_mx(
                out=l2_ps[:],
                lhsT=w2_w[:, 2 * c0 : 2 * (c0 + P)].bitcast(FP4X4),
                lhsT_scale=w2_s[:, c0 : c0 + P],
                rhs=v_w[half][:].bitcast(FP8X4),
                rhs_scale=v_s[half][:],
                start=True,
                stop=True,
            )
            l2 = ring.tile([P, HALF], F32, name="l2", tag="l2", bufs=6)
            nc.scalar.copy(out=l2[:], in_=l2_ps[:])
            l1_ps = bank("l1_ps", HALF, L1_BANKS)
            words, scales = w1_q[g]
            nc.tensor.matmul_mx(
                out=l1_ps[:],
                lhsT=words[:, t * P : (t + 1) * P].bitcast(FP8X4),
                lhsT_scale=scales[:, t * P : (t + 1) * P],
                rhs=v_w[half][:].bitcast(FP8X4),
                rhs_scale=v_s[half][:],
                start=True,
                stop=True,
            )
            if t == 0:
                low[(g, half)] = ring.tile([P, PACK, HALF], F32, name="low", tag="low", bufs=3)
            high[(g, half, t)] = ring.tile([P, HALF], F32, name="high", tag="high", bufs=8)
            nc.vector.tensor_tensor(out=low[(g, half)][:, t, :], in0=l1_ps[:], in1=l2[:], op=ALU.min)
            nc.vector.tensor_tensor(out=high[(g, half, t)][:], in0=l1_ps[:], in1=l2[:], op=ALU.max)

        def cap(g, half, t, c0=0, width=HALF):
            entries = slice(half * HALF + c0, half * HALF + c0 + width)
            l3_ps = bank("l3_ps", width, L3_BANKS)
            for a in range(K2 // PASS):
                words, scales = wx_q[(a, g)]
                nc.tensor.matmul_mx(
                    out=l3_ps[:],
                    lhsT=words[:, t * P : (t + 1) * P].bitcast(FP8X4),
                    lhsT_scale=scales[:, t * P : (t + 1) * P],
                    rhs=xs_w[a][:, entries].bitcast(FP8X4),
                    rhs_scale=xs_s[4 * a : P, entries],
                    start=(a == 0),
                    stop=(a == K2 // PASS - 1),
                )
            if t == 0 and c0 == 0:
                capped[(g, half)] = ring.tile([P, PACK, HALF], F32, name="capped", tag="capped", bufs=2)
            nc.vector.scalar_tensor_tensor(
                out=capped[(g, half)][:, t, c0 : c0 + width],
                in0=l3_ps[:],
                scalar=bias[:, g * PACK + t : g * PACK + t + 1],
                in1=high[(g, half, t)][:, c0 : c0 + width],
                op0=ALU.add,
                op1=ALU.min,
            )

        def vote(g, half, c0, width):
            if c0 == 0:
                h_woven[(g, half)] = ring.tile(
                    [P, PACK * HALF], BF16, name="h_woven", tag="h_woven", bufs=2, align_bytes=64
                )
            by_runs = "p t (c i) -> p c t i"
            nc.vector.tensor_tensor(
                out=h_woven[(g, half)][:, PACK * c0 : PACK * (c0 + width)].rearrange(
                    "p (c i t) -> p c t i", i=RUN, t=PACK
                ),
                in0=low[(g, half)][:, :, c0 : c0 + width].rearrange(by_runs, i=RUN),
                in1=capped[(g, half)][:, :, c0 : c0 + width].rearrange(by_runs, i=RUN),
                op=ALU.max,
            )

        def quantise_h(g, half, c0, width):
            quantise(h_q[(g, half)], h_woven[(g, half)], c0, width)

        def vote_half(g, half, between):
            between(0)
            vote(g, half, 0, QUARTER)
            between(1)
            vote(g, half, QUARTER, QUARTER)
            between(2)
            quantise_h(g, half, 0, HALF)
            between(3)

        def score_pass(y_ps, n, g, half, c0, width):
            columns = slice(g * N + n * P, g * N + (n + 1) * P)
            nc.tensor.matmul_mx(
                out=y_ps[:],
                lhsT=wo_q[0][:, columns].bitcast(FP8X4),
                lhsT_scale=wo_q[1][:, columns],
                rhs=h_q[(g, half)][0][:, c0 : c0 + width].bitcast(FP8X4),
                rhs_scale=h_q[(g, half)][1][:, c0 : c0 + width],
                start=(g == 0),
                stop=(g == GROUPS - 1),
            )

        def open_scores(half, c0, width, banks):
            sums = []
            for n in range(N_TILES):
                y_ps = bank("y_ps", width, banks)
                score_pass(y_ps, n, 0, half, c0, width)
                sums.append(y_ps)
            return sums

        def close_scores(half, c0, width, sums):
            staged = held("staged%d_%d" % (half, c0), [P, N_TILES, width], F32)
            for n in range(N_TILES):
                score_pass(sums[n], n, 1, half, c0, width)
                nc.scalar.activation(
                    out=staged[:, n, :], in_=sums[n][:], func=IDENTITY, bias=bias[:, BO_COLUMN + n : BO_COLUMN + n + 1]
                )
            j0 = half * HALF + c0
            nc.sync.dma_start(out=out[:, j0 : j0 + width].rearrange("(a p) j -> p a j", p=P), in_=staged[:])

        gather_words(0)
        gather_scales(0, "v_s0")
        gather_words(1)
        order_w2_words(0)
        order_w2_scales()
        gather_scales(1, "then_v_s")
        woven = weave_weight(w1_raw[0])
        for t in range(PACK):
            quantise(w1_q[0], woven, t * P, P)
            if t > 0:
                low_high(0, 0, t - 1)
        low_high(0, 0, PACK - 1)
        order_w2_words(1)
        woven = weave_weight(wx_raw[(0, 0)])
        low_high(0, 1, 0)
        quantise(wx_q[(0, 0)], woven, 0, PASS)
        low_high(0, 1, 1)
        woven = weave_weight(wx_raw[(1, 0)])
        low_high(0, 1, 2)
        quantise(wx_q[(1, 0)], woven, 0, PASS)

        identity = ring.tile([P, P], F32, name="identity", tag="then_identity", bufs=1, align_bytes=64)
        make_identity(nc, identity[:])
        bias_ps = bank("bias_ps", P, SCALAR_BANKS)
        nc.tensor.transpose(bias_ps[:], bias_rows[:], identity[:])
        nc.scalar.copy(out=bias[:], in_=bias_ps[:, 0:BIAS_COLUMNS])
        low_high(0, 1, 3)

        woven = weave_weight(w1_raw[1])
        for t in range(PACK):
            cap(0, 0, t)
        quantise(w1_q[1], woven, 0, PASS)
        woven = weave_weight(wx_raw[(0, 1)])
        vote_half(0, 0, lambda t: cap(0, 1, t))
        quantise(wx_q[(0, 1)], woven, 0, PASS)
        woven = weave_weight(wx_raw[(1, 1)])
        vote_half(0, 1, lambda t: low_high(1, 0, t))
        quantise(wx_q[(1, 1)], woven, 0, PASS)

        low_high(1, 1, 0)
        woven = weave_wo()
        for t in range(PACK):
            cap(1, 0, t)
            if t + 1 < PACK:
                low_high(1, 1, t + 1)
        quantise(wo_q, woven, 0, PASS)
        quantise(wo_q, woven, PASS, GROUPS * N - PASS)

        sums = open_scores(0, 0, HALF, SCALAR_BANKS)
        cap(1, 1, 0, 0, QUARTER)
        vote(1, 0, 0, QUARTER)
        cap(1, 1, 1, 0, QUARTER)
        vote(1, 0, QUARTER, QUARTER)
        cap(1, 1, 2, 0, QUARTER)
        quantise_h(1, 0, 0, HALF)
        close_scores(0, 0, HALF, sums)
        cap(1, 1, 3, 0, QUARTER)
        cap(1, 1, 0, QUARTER, QUARTER)
        vote(1, 1, 0, QUARTER)
        sums = open_scores(1, 0, QUARTER, SCALAR_BANKS)
        cap(1, 1, 1, QUARTER, QUARTER)
        quantise_h(1, 1, 0, QUARTER)
        close_scores(1, 0, QUARTER, sums)
        cap(1, 1, 2, QUARTER, QUARTER)
        cap(1, 1, 3, QUARTER, QUARTER)
        last_pieces = [(QUARTER, L3_BANKS), (QUARTER + EIGHTH, SCALAR_BANKS)]
        last_sums = [open_scores(1, c0, EIGHTH, banks) for c0, banks in last_pieces]
        for c0, banks in last_pieces:
            vote(1, 1, c0, EIGHTH)
        for (c0, banks), sums in zip(last_pieces, last_sums):
            quantise_h(1, 1, c0, EIGHTH)
            close_scores(1, c0, EIGHTH, sums)
